import numpy as np
import ml_dtypes


def mxq(x, axis, fmt="e4m3"):
    dtype, down = {"e4m3": (ml_dtypes.float8_e4m3fn, 7), "e5m2": (ml_dtypes.float8_e5m2, 14)}[fmt]
    v = np.moveaxis(np.asarray(x, np.float32).astype(ml_dtypes.bfloat16).astype(np.float64), axis, -1)
    blocks = v.reshape(v.shape[:-1] + (-1, 32))
    amax = np.abs(blocks).max(-1, keepdims=True)
    byte = np.maximum(np.where(amax > 0, np.frexp(amax)[1] - 1 + 127, 0) - down, 1)
    scale = np.exp2(byte - 127.0)
    codes = (blocks / scale).astype(np.float32).astype(dtype).astype(np.float64)
    return np.moveaxis((codes * scale).reshape(v.shape), -1, axis)


WIDE = False


def mx_kscale(k):
    if not WIDE:
        return np.ones(k)
    levels = np.array([30, -30])
    if k % 512:
        return np.exp2(np.random.permutation(np.resize(levels, k // 32))).repeat(32)
    a = np.empty((k // 512, 16))
    for p in range(k // 512):
        a[p, :8] = np.random.permutation(np.resize(levels, 8))
        for g in range(8):
            far = levels[np.abs(levels - a[p, g]) >= 10]
            a[p, g + 8] = far[np.random.randint(len(far))]
    return np.exp2(a.ravel()).repeat(32)


def f64(x):
    return np.asarray(x).astype(np.float64)


def striped(idx):
    return np.tile(np.asarray(idx).reshape(-1, 16).T, (8, 1)).astype(np.uint16)


def unstriped(offs):
    return offs[:16].T.reshape(-1).astype(np.int64)


E2M1 = np.array([0.0, 0.5, 1.0, 1.5, 2.0, 3.0, 4.0, 6.0, -0.0, -0.5, -1.0, -1.5, -2.0, -3.0, -4.0, -6.0])


def pack_weight(w, fmt):
    k, n = w.shape
    w = f64(np.asarray(w, np.float32).astype(ml_dtypes.bfloat16)).reshape(k // 32, 32, n)
    amax = np.abs(w).max(1)
    if fmt in ("e4m3", "e5m2"):
        byte = np.frexp(amax)[1] - 1 + 127 - (7 if fmt == "e4m3" else 14)
    else:
        mant, ex = np.frexp(amax / 6.0)
        byte = np.where(mant > 0.5, ex, ex - 1) + 127
    byte = np.clip(np.where(amax > 0, byte, 1), 1, 254)
    scaled = (w * np.exp2(127.0 - byte)[:, None, :]).reshape(k, n).astype(np.float32)
    by_word = np.ascontiguousarray(scaled.reshape(k // 512, 128, 4, n).transpose(0, 1, 3, 2))
    if fmt in ("e4m3", "e5m2"):
        words = by_word.astype(ml_dtypes.float8_e4m3fn if fmt == "e4m3" else ml_dtypes.float8_e5m2).view(np.uint8)
    else:
        c = by_word.astype(ml_dtypes.float4_e2m1fn).view(np.uint8) & 0xF
        words = (c[..., 0::2] | (c[..., 1::2] << 4)).reshape(k // 512, 128, 2 * n)
    return np.ascontiguousarray(words), np.ascontiguousarray(byte.astype(np.uint8).reshape(k // 512, 16, n))


def unpack_weight(words, scales, fmt):
    g, _, n = scales.shape
    words = np.ascontiguousarray(words).reshape(g, 128, n, -1)
    if fmt in ("e4m3", "e5m2"):
        vals = words.view(ml_dtypes.float8_e4m3fn if fmt == "e4m3" else ml_dtypes.float8_e5m2).astype(np.float64)
    else:
        nib = np.empty((g, 128, n, 4), np.uint8)
        nib[..., 0::2] = words & 0xF
        nib[..., 1::2] = words >> 4
        vals = E2M1[nib]
    vals = vals * np.repeat(np.exp2(scales.astype(np.float64) - 127.0), 8, axis=1)[..., None]
    return vals.transpose(0, 1, 3, 2).reshape(g * 512, n)


K, J, N, R, T, V, Q = 512, 512, 256, 256, 1024, 1024, 1024


def setup_inputs():
    n = np.random.standard_normal
    idx = np.random.permutation(T)[:J]
    idx2 = np.random.permutation(V)[:J]
    idx3 = np.random.permutation(Q)[:N]
    fj = mx_kscale(J)
    fk = mx_kscale(K)
    drp = pack_weight(n((K, R)) * 1 / np.sqrt(K) / fk[:, None], "e5m2")
    return {
        "xf": (n((K, T))).astype(np.float32),
        "ra": (np.random.uniform(0.5, 1.5, (1, J)) * fj).astype(np.float32),
        "lo": (np.random.uniform(-0.3, 0.5, (K, 1))).astype(np.float32),
        "gt": (n((N, V)) * np.exp(0.5 * n((1, V)))).astype(np.float32),
        "rb": (np.random.uniform(0.5, 1.5, (1, J)) / fj).astype(np.float32),
        "pr": (n((N, J))).astype(np.float32),
        "fkr": (np.random.uniform(0.5, 1.5, (1, K)) * fk).astype(np.float32),
        "dr_words": drp[0],
        "dr_scales": drp[1],
        "old": (0.5 * n((R, Q))).astype(np.float32),
        "offs": striped(idx),
        "offs2": striped(idx2),
        "offs3": striped(idx3),
    }


def reference(xf, ra, lo, gt, rb, pr, fkr, dr_words, dr_scales, old, offs, offs2, offs3):
    idx = unstriped(offs)
    idx2 = unstriped(offs2)
    idx3 = unstriped(offs3)
    dru = unpack_weight(dr_words, dr_scales, "e5m2")
    us = np.maximum(f64(xf)[:, idx] - f64(lo), 0.0) * f64(ra)
    ut = us.T
    uj = ut * f64(fkr)
    gs = (f64(gt)[:, idx2] - f64(pr)) * f64(rb)
    gj = gs.T
    ujq = mxq(uj, 0, "e4m3")
    gjq = mxq(gj, 0, "e5m2")
    w = ujq.T @ gjq
    wq = mxq(w, 0, "e5m2")
    v2 = dru.T @ wq
    wp = np.zeros((R, Q))
    wp[:, idx3] = v2
    y = 0.05 * wp + f64(old)
    return y

@@ -1,0 +1,175 @@
+from contextlib import ExitStack
+
+import concourse.mybir as mybir
+from concourse.masks import make_identity
+
+K, J, N, R, T, V, Q = 512, 512, 256, 256, 1024, 1024, 1024
+FLOPS = 2 * J * K * N + 2 * K * R * N
+
+F32 = mybir.dt.float32
+BF16 = mybir.dt.bfloat16
+I32 = mybir.dt.int32
+U32 = mybir.dt.uint32
+U16 = mybir.dt.uint16
+U8 = mybir.dt.uint8
+E4M3 = mybir.dt.float8_e4m3fn_x4
+E5M2 = mybir.dt.float8_e5m2_x4
+ALU = mybir.AluOpType
+COPY = mybir.ActivationFunctionType.Copy
+
+P = 128
+PACK = 4
+STEP = 0.05
+OUT_CHUNK = 512
+
+
+def tile_list_directions_over_errors_placed_kernel(
+    tc, xf, ra, lo, gt, rb, pr, fkr, dr_words, dr_scales, old, offs, offs2, offs3, out
+):
+    nc = tc.nc
+    with ExitStack() as ctx:
+        sb = ctx.enter_context(tc.tile_pool(name="sb", bufs=1))
+        ps = ctx.enter_context(tc.psum_pool(name="ps", bufs=1))
+
+        def load(queue, name, shape, dtype, src):
+            dst = sb.tile(shape, dtype, name=name, tag=name, align_bytes=64)
+            queue.dma_start(out=dst[:], in_=src)
+            return dst
+
+        ident = sb.tile([P, P], F32, name="ident")
+        nc.vector.memset(ident[:], 0.0)
+        make_identity(nc, ident[:], nomemset=True)
+        placed = [sb.tile([P, Q], F32, name="placed%d" % h) for h in range(2)]
+        for h in range(2):
+            nc.vector.memset(placed[h][:], 0.0)
+        dr_plane = sb.tile([P, R], U8, name="dr_plane", align_bytes=64)
+        nc.vector.memset(dr_plane[:].bitcast(U32), 0)
+
+
+        xf_rows = xf.rearrange("(p t) c -> t p c", t=PACK)
+        x_win, pr_sb, g_win = {}, {}, {}
+        fk_col = load(nc.sync, "fk_col", [P, PACK], F32, fkr.rearrange("o (p t) -> p (o t)", t=PACK))
+        ra_col = load(nc.sync, "ra_col", [P, PACK], F32, ra.rearrange("o (p s) -> p (o s)", s=PACK))
+        x_list = load(nc.sync, "x_list", [P, J // 16], U16, offs)
+        x_win[0] = load(nc.sync, "x_win0", [P, T], F32, xf_rows[0])
+        lo_col = load(nc.sync, "lo_col", [P, PACK], F32, lo.rearrange("(p t) o -> p (t o)", t=PACK))
+        x_win[1] = load(nc.sync, "x_win1", [P, T], F32, xf_rows[1])
+        x_win[2] = load(nc.sync, "x_win2", [P, T], F32, xf_rows[2])
+        x_win[3] = load(nc.sync, "x_win3", [P, T], F32, xf_rows[3])
+        g_list = load(nc.sync, "g_list", [P, J // 16], U16, offs2)
+        rb_col = load(nc.sync, "rb_col", [P, PACK], F32, rb.rearrange("o (p s) -> p (o s)", s=PACK))
+        pr_sb[0] = load(nc.sync, "pr0", [P, J], F32, pr[0 * P : 1 * P, :])
+        g_win[0] = load(nc.sync, "g_win0", [P, V], F32, gt[0 * P : 1 * P, :])
+        pr_sb[1] = load(nc.sync, "pr1", [P, J], F32, pr[1 * P : 2 * P, :])
+        g_win[1] = load(nc.sync, "g_win1", [P, V], F32, gt[1 * P : 2 * P, :])
+        dr_codes = load(nc.sync, "dr_codes", [P, R], I32, dr_words[0].rearrange("p c t -> p (c t)").bitcast(I32))
+        for quad in range(4):
+            nc.sync.dma_start(
+                out=dr_plane[32 * quad : 32 * quad + 4, :].bitcast(I32),
+                in_=dr_scales[0, 4 * quad : 4 * quad + 4, :].bitcast(I32),
+            )
+        out_list = load(nc.sync, "out_list", [P, N // 16], U16, offs3)
+        old_sb = [load(nc.sync, "old%d" % h, [P, Q], F32, old[h * P : (h + 1) * P, :]) for h in range(2)]
+
+        fk_all = ps.tile([P, PACK, P], F32, name="fk_all", tag="early")
+        for t in range(PACK):
+            nc.tensor.transpose(fk_all[:, t, :], fk_col[:, t : t + 1].to_broadcast([P, P]), ident[:])
+
+        def by_slot(tile):
+            return tile[:].rearrange("p (m s) -> p m s", s=PACK)
+
+        def along_columns(col):
+            return col[:].rearrange("p (o s) -> p o s", o=1).to_broadcast([P, P, PACK])
+
+        factor = []
+        for t in range(PACK):
+            both = sb.tile([P, P * PACK], F32, name="factor%d" % t)
+            nc.vector.tensor_tensor(
+                by_slot(both),
+                fk_all[:, t, :].rearrange("p (m o) -> p m o", o=1).to_broadcast([P, P, PACK]),
+                along_columns(ra_col),
+                ALU.mult,
+            )
+            factor.append(both)
+
+        neg_lo = sb.tile([P, PACK], F32, name="neg_lo", tag="ra_col", align_bytes=64)
+        nc.vector.tensor_scalar(neg_lo[:], lo_col[:], -1.0, None, ALU.mult)
+
+        def quantize(grouped, name, fmt):
+            codes = sb.tile([P, P], U32, name=name + "_codes", align_bytes=64)
+            plane = sb.tile([P, P], U8, name=name + "_plane", align_bytes=64)
+            nc.vector.quantize_mx(out=codes[:].bitcast(fmt), scales=plane[:], in_=grouped[:])
+            return codes, plane
+
+        u_mx = []
+        for t in range(PACK):
+            picked = sb.tile([P, J], F32, name="x_picked%d" % t, tag="picked", bufs=2)
+            nc.scalar.activation(picked[:], x_win[t][:].indirect(x_list[:]), COPY)
+            excess = sb.tile([P, PACK, P], F32, name="excess%d" % t, tag="excess", bufs=2)
+            nc.vector.tensor_scalar(
+                excess[:].rearrange("m s p -> m p s"), by_slot(picked), neg_lo[:, t : t + 1], 0.0, ALU.add, ALU.max
+            )
+            u_bank = ps.tile([P, PACK, P], F32, name="u_bank%d" % t, tag="turn%d" % (t % 3))
+            for s in range(PACK):
+                nc.tensor.transpose(u_bank[:, s, :], excess[:, s, :], ident[:])
+            u_bf = sb.tile([P, P * PACK], BF16, name="u_bf%d" % t, align_bytes=64)
+            nc.vector.tensor_tensor(
+                by_slot(u_bf), u_bank[:].rearrange("p s m -> p m s"), by_slot(factor[t]), ALU.mult
+            )
+            u_mx.append(quantize(u_bf, "u%d" % t, E4M3))
+
+        g_mx = []
+        for h in range(2):
+            g_bank = ps.tile([P, PACK, P], F32, name="g_bank%d" % h, tag="turn%d" % (h + 1))
+            for s in range(PACK):
+                nc.tensor.matmul(
+                    g_bank[:, s, :], pr_sb[h][:, s::PACK], ident[:], is_transpose=True, start=(s == 0), stop=False
+                )
+            negated = sb.tile([P, J], F32, name="g_negated%d" % h, tag="picked", bufs=2)
+            nc.scalar.activation(negated[:], g_win[h][:].indirect(g_list[:]), COPY, scale=-1.0)
+            for s in range(PACK):
+                nc.tensor.matmul(
+                    g_bank[:, s, :], negated[:, s::PACK], ident[:], is_transpose=True, start=False, stop=(s == PACK - 1)
+                )
+            g_bf = sb.tile([P, P * PACK], BF16, name="g_bf%d" % h, align_bytes=64)
+            nc.vector.scalar_tensor_tensor(
+                by_slot(g_bf), g_bank[:].rearrange("p s m -> p m s"), -1.0, along_columns(rb_col), ALU.mult, ALU.mult
+            )
+            g_mx.append(quantize(g_bf, "g%d" % h, E5M2))
+
+        for h in range(2):
+            g_codes, g_plane = g_mx[h]
+            w_bank = ps.tile([P, PACK, P], F32, name="w_bank%d" % h, tag="early" if h == 0 else "late")
+            for t in range(PACK):
+                u_codes, u_plane = u_mx[t]
+                nc.tensor.matmul_mx(
+                    out=w_bank[:, t, :], lhsT=u_codes[:].bitcast(E4M3), lhsT_scale=u_plane[:],
+                    rhs=g_codes[:].bitcast(E5M2), rhs_scale=g_plane[:], start=True, stop=True,
+                )
+            w_bf = sb.tile([P, P * PACK], BF16, name="w_bf%d" % h, align_bytes=64)
+            nc.scalar.copy(out=by_slot(w_bf), in_=w_bank[:].rearrange("p t n -> p n t"))
+            w_codes, w_plane = quantize(w_bf, "w%d" % h, E5M2)
+            places = out_list[:, h * (P // 16) : (h + 1) * (P // 16)]
+            for b in range(2):
+                v_bank = ps.tile([P, P], F32, name="v_bank%d_%d" % (h, b), tag="v%d" % b)
+                nc.tensor.matmul_mx(
+                    out=v_bank[:], lhsT=dr_codes[:, b * P : (b + 1) * P].bitcast(E5M2),
+                    lhsT_scale=dr_plane[:, b * P : (b + 1) * P],
+                    rhs=w_codes[:].bitcast(E5M2), rhs_scale=w_plane[:], start=True, stop=True,
+                )
+                v_sb = sb.tile([P, P], F32, name="v_sb%d_%d" % (h, b))
+                if b == 0:
+                    nc.vector.tensor_copy(v_sb[:], v_bank[:])
+                    nc.vector.tensor_copy(placed[b][:].indirect(places), v_sb[:])
+                else:
+                    nc.scalar.copy(out=v_sb[:], in_=v_bank[:])
+                    nc.scalar.activation(placed[b][:].indirect(places), v_sb[:], COPY)
+
+        for b in range(2):
+            for c0 in range(0, Q, OUT_CHUNK):
+                cols = slice(c0, c0 + OUT_CHUNK)
+                result = sb.tile([P, OUT_CHUNK], F32, name="result%d_%d" % (b, c0))
+                nc.vector.scalar_tensor_tensor(
+                    result[:], placed[b][:, cols], STEP, old_sb[b][:, cols], ALU.mult, ALU.add
+                )
+                nc.sync.dma_start(out=out[b * P : (b + 1) * P, cols], in_=result[:])

@@ -36,6 +36,9 @@ def tile_list_directions_over_errors_placed_kernel(
             queue.dma_start(out=dst[:], in_=src)
             return dst
 
+        warm = sb.tile([P, 2], F32, name="warm")
+        nc.vector.memset(warm[:, 0:1], 0.0)
+        nc.scalar.activation(warm[:, 1:2], warm[:, 0:1], COPY)
         ident = sb.tile([P, P], F32, name="ident")
         nc.vector.memset(ident[:], 0.0)
         make_identity(nc, ident[:], nomemset=True)

@@ -19,8 +19,11 @@ COPY = mybir.ActivationFunctionType.Copy
 
 P = 128
 PACK = 4
+HALVES = 2
+LIST_ROWS = 16
+QUADRANTS = 4
 STEP = 0.05
-OUT_CHUNK = 512
+STORE_COLUMNS = 512
 
 
 def tile_list_directions_over_errors_placed_kernel(
@@ -28,151 +31,165 @@ def tile_list_directions_over_errors_placed_kernel(
 ):
     nc = tc.nc
     with ExitStack() as ctx:
-        sb = ctx.enter_context(tc.tile_pool(name="sb", bufs=1))
-        ps = ctx.enter_context(tc.psum_pool(name="ps", bufs=1))
+        sbuf = ctx.enter_context(tc.tile_pool(name="sbuf", bufs=1))
+        psum = ctx.enter_context(tc.psum_pool(name="psum", bufs=1))
 
-        def load(queue, name, shape, dtype, src):
-            dst = sb.tile(shape, dtype, name=name, tag=name, align_bytes=64)
-            queue.dma_start(out=dst[:], in_=src)
-            return dst
+        def tile(name, columns, dtype, tag=None, bufs=1):
+            return sbuf.tile([P, columns], dtype, name=name, tag=tag or name, bufs=bufs, align_bytes=64)
 
-        warm = sb.tile([P, 2], F32, name="warm")
+        def bank(name, tag):
+            return psum.tile([P, PACK, P], F32, name=name, tag=tag)
+
+        def load(name, columns, dtype, source):
+            loaded = tile(name, columns, dtype)
+            nc.sync.dma_start(out=loaded[:], in_=source)
+            return loaded
+
+        def in_fours(ap):
+            return ap.rearrange("p (c s) -> p c s", s=PACK)
+
+        def dealt(ap):
+            return ap.rearrange("p (s c) -> p c s", s=PACK)
+
+        def per_byte(weights):
+            return weights[:].rearrange("p (o s) -> p o s", o=1).to_broadcast([P, P, PACK])
+
+        warm = tile("warm", 2, F32)
         nc.vector.memset(warm[:, 0:1], 0.0)
         nc.scalar.activation(warm[:, 1:2], warm[:, 0:1], COPY)
-        ident = sb.tile([P, P], F32, name="ident")
-        nc.vector.memset(ident[:], 0.0)
-        make_identity(nc, ident[:], nomemset=True)
-        placed = [sb.tile([P, Q], F32, name="placed%d" % h) for h in range(2)]
-        for h in range(2):
-            nc.vector.memset(placed[h][:], 0.0)
-        dr_plane = sb.tile([P, R], U8, name="dr_plane", align_bytes=64)
-        nc.vector.memset(dr_plane[:].bitcast(U32), 0)
 
+        identity = tile("identity", P, F32)
+        nc.vector.memset(identity[:], 0.0)
+        make_identity(nc, identity[:], nomemset=True)
+        placed = [tile("placed%d" % b, Q, F32) for b in range(HALVES)]
+        for b in range(HALVES):
+            nc.vector.memset(placed[b][:], 0.0)
+        dr_scale = tile("dr_scale", R, U8)
+        nc.vector.memset(dr_scale[:].bitcast(U32), 0)
 
-        xf_rows = xf.rearrange("(p t) c -> t p c", t=PACK)
-        x_win, pr_sb, g_win = {}, {}, {}
-        fk_col = load(nc.sync, "fk_col", [P, PACK], F32, fkr.rearrange("o (p t) -> p (o t)", t=PACK))
-        ra_col = load(nc.sync, "ra_col", [P, PACK], F32, ra.rearrange("o (p s) -> p (o s)", s=PACK))
-        x_list = load(nc.sync, "x_list", [P, J // 16], U16, offs)
-        x_win[0] = load(nc.sync, "x_win0", [P, T], F32, xf_rows[0])
-        lo_col = load(nc.sync, "lo_col", [P, PACK], F32, lo.rearrange("(p t) o -> p (t o)", t=PACK))
-        x_win[1] = load(nc.sync, "x_win1", [P, T], F32, xf_rows[1])
-        x_win[2] = load(nc.sync, "x_win2", [P, T], F32, xf_rows[2])
-        x_win[3] = load(nc.sync, "x_win3", [P, T], F32, xf_rows[3])
-        g_list = load(nc.sync, "g_list", [P, J // 16], U16, offs2)
-        rb_col = load(nc.sync, "rb_col", [P, PACK], F32, rb.rearrange("o (p s) -> p (o s)", s=PACK))
-        pr_sb[0] = load(nc.sync, "pr0", [P, J], F32, pr[0 * P : 1 * P, :])
-        g_win[0] = load(nc.sync, "g_win0", [P, V], F32, gt[0 * P : 1 * P, :])
-        pr_sb[1] = load(nc.sync, "pr1", [P, J], F32, pr[1 * P : 2 * P, :])
-        g_win[1] = load(nc.sync, "g_win1", [P, V], F32, gt[1 * P : 2 * P, :])
-        dr_codes = load(nc.sync, "dr_codes", [P, R], I32, dr_words[0].rearrange("p c t -> p (c t)").bitcast(I32))
-        for quad in range(4):
+        fk_col = load("fk_col", PACK, F32, fkr.rearrange("o (m t) -> m (o t)", t=PACK))
+        ra_col = load("ra_col", PACK, F32, ra.rearrange("o (p s) -> p (o s)", s=PACK))
+        x_list = load("x_list", J // LIST_ROWS, U16, offs)
+        xf_tiles = xf.rearrange("(m t) c -> t m c", t=PACK)
+        x_table = [load("x_table0", T, F32, xf_tiles[0])]
+        lo_col = load("lo_col", PACK, F32, lo.rearrange("(m t) o -> m (t o)", t=PACK))
+        x_table.extend(load("x_table%d" % t, T, F32, xf_tiles[t]) for t in range(1, PACK))
+        g_list = load("g_list", J // LIST_ROWS, U16, offs2)
+        rb_col = load("rb_col", PACK, F32, rb.rearrange("o (p s) -> p (o s)", s=PACK))
+        g_table, prediction = [], []
+        for h in range(HALVES):
+            g_table.append(load("g_table%d" % h, V, F32, gt[h * P : (h + 1) * P, :]))
+            prediction.append(load("prediction%d" % h, J, F32, pr[h * P : (h + 1) * P, :]))
+        dr_code = load("dr_code", R, I32, dr_words[0].rearrange("p c s -> p (c s)").bitcast(I32))
+        for quadrant in range(QUADRANTS):
             nc.sync.dma_start(
-                out=dr_plane[32 * quad : 32 * quad + 4, :].bitcast(I32),
-                in_=dr_scales[0, 4 * quad : 4 * quad + 4, :].bitcast(I32),
+                out=dr_scale[32 * quadrant : 32 * quadrant + 4, :].bitcast(I32),
+                in_=dr_scales[0, 4 * quadrant : 4 * quadrant + 4, :].bitcast(I32),
             )
-        out_list = load(nc.sync, "out_list", [P, N // 16], U16, offs3)
-        old_sb = [load(nc.sync, "old%d" % h, [P, Q], F32, old[h * P : (h + 1) * P, :]) for h in range(2)]
-
-        fk_all = ps.tile([P, PACK, P], F32, name="fk_all", tag="early")
-        for t in range(PACK):
-            nc.tensor.transpose(fk_all[:, t, :], fk_col[:, t : t + 1].to_broadcast([P, P]), ident[:])
-
-        def by_slot(tile):
-            return tile[:].rearrange("p (m s) -> p m s", s=PACK)
-
-        def along_columns(col):
-            return col[:].rearrange("p (o s) -> p o s", o=1).to_broadcast([P, P, PACK])
+        out_list = load("out_list", N // LIST_ROWS, U16, offs3)
+        old_rows = [load("old_rows%d" % b, Q, F32, old[b * P : (b + 1) * P, :]) for b in range(HALVES)]
 
         factor = []
         for t in range(PACK):
-            both = sb.tile([P, P * PACK], F32, name="factor%d" % t)
+            spread = psum.tile([P, P], F32, name="spread%d" % t, tag="bank%d" % t)
+            nc.tensor.transpose(spread[:], fk_col[:, t : t + 1].to_broadcast([P, P]), identity[:])
+            factor.append(tile("factor%d" % t, P * PACK, F32))
             nc.vector.tensor_tensor(
-                by_slot(both),
-                fk_all[:, t, :].rearrange("p (m o) -> p m o", o=1).to_broadcast([P, P, PACK]),
-                along_columns(ra_col),
+                in_fours(factor[t][:]),
+                spread[:].rearrange("p (m o) -> p m o", o=1).to_broadcast([P, P, PACK]),
+                per_byte(ra_col),
                 ALU.mult,
             )
-            factor.append(both)
+        minus_lo = tile("minus_lo", PACK, F32, tag="ra_col")
+        nc.vector.tensor_scalar(minus_lo[:], lo_col[:], -1.0, None, ALU.mult)
 
-        neg_lo = sb.tile([P, PACK], F32, name="neg_lo", tag="ra_col", align_bytes=64)
-        nc.vector.tensor_scalar(neg_lo[:], lo_col[:], -1.0, None, ALU.mult)
+        def gather(name, table, offsets):
+            picked = tile(name, J, F32)
+            nc.scalar.activation(picked[:], table[:].indirect(offsets[:]), COPY)
+            return picked
 
-        def quantize(grouped, name, fmt):
-            codes = sb.tile([P, P], U32, name=name + "_codes", align_bytes=64)
-            plane = sb.tile([P, P], U8, name=name + "_plane", align_bytes=64)
-            nc.vector.quantize_mx(out=codes[:].bitcast(fmt), scales=plane[:], in_=grouped[:])
-            return codes, plane
+        x_picked = [gather("x_picked%d" % t, x_table[t], x_list) for t in range(PACK)]
+        g_picked = [gather("g_picked%d" % h, g_table[h], g_list) for h in range(HALVES)]
 
+        def turn(parts, name, tag):
+            turned = bank(name, tag)
+            for s in range(PACK):
+                nc.tensor.transpose(turned[:, s, :], parts[:, s * P : (s + 1) * P], identity[:])
+            return turned
+
+        def turn_excess(t):
+            excess = tile("excess%d" % t, J, F32, tag="excess", bufs=2)
+            nc.vector.tensor_scalar(
+                dealt(excess[:]), in_fours(x_picked[t][:]), minus_lo[:, t : t + 1], 0.0, ALU.add, ALU.max
+            )
+            return turn(excess, "excess_turned%d" % t, "bank%d" % t)
+
+        def turn_error(h):
+            error = tile("error%d" % h, J, F32, tag="factor%d" % (PACK - HALVES + h))
+            nc.vector.tensor_tensor(dealt(error[:]), in_fours(g_picked[h][:]), in_fours(prediction[h][:]), ALU.subtract)
+            return turn(error, "error_turned%d" % h, "bank%d" % h)
+
+        def weigh(turned, weights, name, tag=None):
+            rounded = tile(name, P * PACK, BF16, tag=tag)
+            nc.vector.tensor_tensor(in_fours(rounded[:]), turned[:].rearrange("p s c -> p c s"), weights, ALU.mult)
+            return rounded
+
+        def quantize(rounded, name, fmt):
+            code = tile(name + "_code", P, U32)
+            scale = tile(name + "_scale", P, U8)
+            nc.vector.quantize_mx(out=code[:].bitcast(fmt), scales=scale[:], in_=rounded[:])
+            return code[:].bitcast(fmt), scale[:]
+
+        prepare = [lambda t=t: turn_excess(t) for t in range(PACK)] + [lambda h=h: turn_error(h) for h in range(HALVES)]
+        turned = [prepare[0](), prepare[1]()]
         u_mx = []
         for t in range(PACK):
-            picked = sb.tile([P, J], F32, name="x_picked%d" % t, tag="picked", bufs=2)
-            nc.scalar.activation(picked[:], x_win[t][:].indirect(x_list[:]), COPY)
-            excess = sb.tile([P, PACK, P], F32, name="excess%d" % t, tag="excess", bufs=2)
-            nc.vector.tensor_scalar(
-                excess[:].rearrange("m s p -> m p s"), by_slot(picked), neg_lo[:, t : t + 1], 0.0, ALU.add, ALU.max
-            )
-            u_bank = ps.tile([P, PACK, P], F32, name="u_bank%d" % t, tag="turn%d" % (t % 3))
-            for s in range(PACK):
-                nc.tensor.transpose(u_bank[:, s, :], excess[:, s, :], ident[:])
-            u_bf = sb.tile([P, P * PACK], BF16, name="u_bf%d" % t, align_bytes=64)
-            nc.vector.tensor_tensor(
-                by_slot(u_bf), u_bank[:].rearrange("p s m -> p m s"), by_slot(factor[t]), ALU.mult
-            )
-            u_mx.append(quantize(u_bf, "u%d" % t, E4M3))
-
+            rounded = weigh(turned[t], in_fours(factor[t][:]), "u_rounded%d" % t)
+            turned.append(prepare[t + 2]())
+            u_mx.append(quantize(rounded, "u%d" % t, E4M3))
         g_mx = []
-        for h in range(2):
-            g_bank = ps.tile([P, PACK, P], F32, name="g_bank%d" % h, tag="turn%d" % (h + 1))
-            for s in range(PACK):
-                nc.tensor.matmul(
-                    g_bank[:, s, :], pr_sb[h][:, s::PACK], ident[:], is_transpose=True, start=(s == 0), stop=False
-                )
-            negated = sb.tile([P, J], F32, name="g_negated%d" % h, tag="picked", bufs=2)
-            nc.scalar.activation(negated[:], g_win[h][:].indirect(g_list[:]), COPY, scale=-1.0)
-            for s in range(PACK):
-                nc.tensor.matmul(
-                    g_bank[:, s, :], negated[:, s::PACK], ident[:], is_transpose=True, start=False, stop=(s == PACK - 1)
-                )
-            g_bf = sb.tile([P, P * PACK], BF16, name="g_bf%d" % h, align_bytes=64)
-            nc.vector.scalar_tensor_tensor(
-                by_slot(g_bf), g_bank[:].rearrange("p s m -> p m s"), -1.0, along_columns(rb_col), ALU.mult, ALU.mult
-            )
-            g_mx.append(quantize(g_bf, "g%d" % h, E5M2))
+        for h in range(HALVES):
+            rounded = weigh(turned[PACK + h], per_byte(rb_col), "g_rounded%d" % h, tag="g_rounded")
+            g_mx.append(quantize(rounded, "g%d" % h, E5M2))
 
-        for h in range(2):
-            g_codes, g_plane = g_mx[h]
-            w_bank = ps.tile([P, PACK, P], F32, name="w_bank%d" % h, tag="early" if h == 0 else "late")
+        second_rows = psum.tile([P, N], F32, name="second_rows")
+        for h in range(HALVES):
+            copy = nc.scalar.copy if h == 0 else nc.vector.tensor_copy
+            g_code, g_scale = g_mx[h]
+            moment = bank("moment%d" % h, "bank%d" % (PACK - HALVES + h))
             for t in range(PACK):
-                u_codes, u_plane = u_mx[t]
+                u_code, u_scale = u_mx[t]
                 nc.tensor.matmul_mx(
-                    out=w_bank[:, t, :], lhsT=u_codes[:].bitcast(E4M3), lhsT_scale=u_plane[:],
-                    rhs=g_codes[:].bitcast(E5M2), rhs_scale=g_plane[:], start=True, stop=True,
+                    out=moment[:, t, :], lhsT=u_code, lhsT_scale=u_scale, rhs=g_code, rhs_scale=g_scale,
+                    start=True, stop=True,
                 )
-            w_bf = sb.tile([P, P * PACK], BF16, name="w_bf%d" % h, align_bytes=64)
-            nc.scalar.copy(out=by_slot(w_bf), in_=w_bank[:].rearrange("p t n -> p n t"))
-            w_codes, w_plane = quantize(w_bf, "w%d" % h, E5M2)
-            places = out_list[:, h * (P // 16) : (h + 1) * (P // 16)]
-            for b in range(2):
-                v_bank = ps.tile([P, P], F32, name="v_bank%d_%d" % (h, b), tag="v%d" % b)
+            w_rounded = tile("w_rounded%d" % h, P * PACK, BF16)
+            copy(out=in_fours(w_rounded[:]), in_=moment[:].rearrange("p t n -> p n t"))
+            w_code, w_scale = quantize(w_rounded, "w%d" % h, E5M2)
+            first_rows = psum.tile([P, P], F32, name="first_rows%d" % h)
+            for b, seen in enumerate((first_rows[:], second_rows[:, h * P : (h + 1) * P])):
                 nc.tensor.matmul_mx(
-                    out=v_bank[:], lhsT=dr_codes[:, b * P : (b + 1) * P].bitcast(E5M2),
-                    lhsT_scale=dr_plane[:, b * P : (b + 1) * P],
-                    rhs=w_codes[:].bitcast(E5M2), rhs_scale=w_plane[:], start=True, stop=True,
+                    out=seen,
+                    lhsT=dr_code[:, b * P : (b + 1) * P].bitcast(E5M2),
+                    lhsT_scale=dr_scale[:, b * P : (b + 1) * P],
+                    rhs=w_code, rhs_scale=w_scale, start=True, stop=True,
                 )
-                v_sb = sb.tile([P, P], F32, name="v_sb%d_%d" % (h, b))
-                if b == 0:
-                    nc.vector.tensor_copy(v_sb[:], v_bank[:])
-                    nc.vector.tensor_copy(placed[b][:].indirect(places), v_sb[:])
-                else:
-                    nc.scalar.copy(out=v_sb[:], in_=v_bank[:])
-                    nc.scalar.activation(placed[b][:].indirect(places), v_sb[:], COPY)
+            first_values = tile("first_values%d" % h, P, F32)
+            copy(out=first_values[:], in_=first_rows[:])
+            places = placed[0][:].indirect(out_list[:, h * P // LIST_ROWS : (h + 1) * P // LIST_ROWS])
+            if h == 0:
+                nc.scalar.activation(places, first_values[:], COPY)
+            else:
+                nc.vector.tensor_copy(places, first_values[:])
+        second_values = tile("second_values", N, F32)
+        nc.scalar.copy(out=second_values[:], in_=second_rows[:])
+        nc.scalar.activation(placed[1][:].indirect(out_list[:]), second_values[:], COPY)
 
-        for b in range(2):
-            for c0 in range(0, Q, OUT_CHUNK):
-                cols = slice(c0, c0 + OUT_CHUNK)
-                result = sb.tile([P, OUT_CHUNK], F32, name="result%d_%d" % (b, c0))
+        for b in range(HALVES):
+            for first in range(0, Q, STORE_COLUMNS):
+                columns = slice(first, first + STORE_COLUMNS)
+                result = tile("result%d_%d" % (b, first), STORE_COLUMNS, F32)
                 nc.vector.scalar_tensor_tensor(
-                    result[:], placed[b][:, cols], STEP, old_sb[b][:, cols], ALU.mult, ALU.add
+                    result[:], placed[b][:, columns], STEP, old_rows[b][:, columns], ALU.mult, ALU.add
                 )
-                nc.sync.dma_start(out=out[b * P : (b + 1) * P, cols], in_=result[:])
+                nc.sync.dma_start(out=out[b * P : (b + 1) * P, columns], in_=result[:])

@@ -40,9 +40,9 @@ def tile_list_directions_over_errors_placed_kernel(
         def bank(name, tag):
             return psum.tile([P, PACK, P], F32, name=name, tag=tag)
 
-        def load(name, columns, dtype, source):
+        def load(name, columns, dtype, source, queue=nc.sync):
             loaded = tile(name, columns, dtype)
-            nc.sync.dma_start(out=loaded[:], in_=source)
+            queue.dma_start(out=loaded[:], in_=source)
             return loaded
 
         def in_fours(ap):
@@ -56,30 +56,27 @@ def tile_list_directions_over_errors_placed_kernel(
 
         warm = tile("warm", 2, F32)
         nc.vector.memset(warm[:, 0:1], 0.0)
-        nc.scalar.activation(warm[:, 1:2], warm[:, 0:1], COPY)
 
         identity = tile("identity", P, F32)
         nc.vector.memset(identity[:], 0.0)
         make_identity(nc, identity[:], nomemset=True)
+        dr_scale = tile("dr_scale", R, U8)
+        nc.vector.memset(dr_scale[:].bitcast(U32), 0)
         placed = [tile("placed%d" % b, Q, F32) for b in range(HALVES)]
         for b in range(HALVES):
             nc.vector.memset(placed[b][:], 0.0)
-        dr_scale = tile("dr_scale", R, U8)
-        nc.vector.memset(dr_scale[:].bitcast(U32), 0)
 
-        fk_col = load("fk_col", PACK, F32, fkr.rearrange("o (m t) -> m (o t)", t=PACK))
-        ra_col = load("ra_col", PACK, F32, ra.rearrange("o (p s) -> p (o s)", s=PACK))
+        fk_col = load("fk_col", PACK, F32, fkr.rearrange("o (m t) -> m (o t)", t=PACK), nc.scalar)
+        ra_col = load("ra_col", PACK, F32, ra.rearrange("o (p s) -> p (o s)", s=PACK), nc.scalar)
+        lo_col = load("lo_col", PACK, F32, lo.rearrange("(m t) o -> m (t o)", t=PACK), nc.scalar)
+        rb_col = load("rb_col", PACK, F32, rb.rearrange("o (p s) -> p (o s)", s=PACK), nc.scalar)
+        nc.scalar.activation(warm[:, 1:2], warm[:, 0:1], COPY)
         x_list = load("x_list", J // LIST_ROWS, U16, offs)
         xf_tiles = xf.rearrange("(m t) c -> t m c", t=PACK)
-        x_table = [load("x_table0", T, F32, xf_tiles[0])]
-        lo_col = load("lo_col", PACK, F32, lo.rearrange("(m t) o -> m (t o)", t=PACK))
-        x_table.extend(load("x_table%d" % t, T, F32, xf_tiles[t]) for t in range(1, PACK))
+        x_table = [load("x_table%d" % t, T, F32, xf_tiles[t]) for t in range(PACK)]
         g_list = load("g_list", J // LIST_ROWS, U16, offs2)
-        rb_col = load("rb_col", PACK, F32, rb.rearrange("o (p s) -> p (o s)", s=PACK))
-        g_table, prediction = [], []
-        for h in range(HALVES):
-            g_table.append(load("g_table%d" % h, V, F32, gt[h * P : (h + 1) * P, :]))
-            prediction.append(load("prediction%d" % h, J, F32, pr[h * P : (h + 1) * P, :]))
+        g_table = [load("g_table%d" % h, V, F32, gt[h * P : (h + 1) * P, :]) for h in range(HALVES)]
+        prediction = [load("prediction%d" % h, J, F32, pr[h * P : (h + 1) * P, :]) for h in range(HALVES)]
         dr_code = load("dr_code", R, I32, dr_words[0].rearrange("p c s -> p (c s)").bitcast(I32))
         for quadrant in range(QUADRANTS):
             nc.sync.dma_start(
@@ -118,14 +115,14 @@ def tile_list_directions_over_errors_placed_kernel(
             return turned
 
         def turn_excess(t):
-            excess = tile("excess%d" % t, J, F32, tag="excess", bufs=2)
+            excess = tile("excess%d" % t, J, F32, tag="dealt", bufs=2)
             nc.vector.tensor_scalar(
                 dealt(excess[:]), in_fours(x_picked[t][:]), minus_lo[:, t : t + 1], 0.0, ALU.add, ALU.max
             )
             return turn(excess, "excess_turned%d" % t, "bank%d" % t)
 
         def turn_error(h):
-            error = tile("error%d" % h, J, F32, tag="factor%d" % (PACK - HALVES + h))
+            error = tile("error%d" % h, J, F32, tag="dealt", bufs=2)
             nc.vector.tensor_tensor(dealt(error[:]), in_fours(g_picked[h][:]), in_fours(prediction[h][:]), ALU.subtract)
             return turn(error, "error_turned%d" % h, "bank%d" % h)
 

@@ -111,7 +111,7 @@ def tile_list_directions_over_errors_placed_kernel(
         def turn(parts, name, tag):
             turned = bank(name, tag)
             for s in range(PACK):
-                nc.tensor.transpose(turned[:, s, :], parts[:, s * P : (s + 1) * P], identity[:])
+                nc.tensor.transpose(turned[:, s, :], parts[s], identity[:])
             return turned
 
         def turn_excess(t):
@@ -119,12 +119,12 @@ def tile_list_directions_over_errors_placed_kernel(
             nc.vector.tensor_scalar(
                 dealt(excess[:]), in_fours(x_picked[t][:]), minus_lo[:, t : t + 1], 0.0, ALU.add, ALU.max
             )
-            return turn(excess, "excess_turned%d" % t, "bank%d" % t)
+            return turn([excess[:, s * P : (s + 1) * P] for s in range(PACK)], "excess_turned%d" % t, "bank%d" % t)
 
         def turn_error(h):
             error = tile("error%d" % h, J, F32, tag="dealt", bufs=2)
-            nc.vector.tensor_tensor(dealt(error[:]), in_fours(g_picked[h][:]), in_fours(prediction[h][:]), ALU.subtract)
-            return turn(error, "error_turned%d" % h, "bank%d" % h)
+            nc.vector.tensor_tensor(error[:], g_picked[h][:], prediction[h][:], ALU.subtract)
+            return turn([error[:, s::PACK] for s in range(PACK)], "error_turned%d" % h, "bank%d" % h)
 
         def weigh(turned, weights, name, tag=None):
             rounded = tile(name, P * PACK, BF16, tag=tag)

from contextlib import ExitStack

import concourse.mybir as mybir
from concourse.masks import make_identity

K, J, N, R, T, V, Q = 512, 512, 256, 256, 1024, 1024, 1024
FLOPS = 2 * J * K * N + 2 * K * R * N

F32 = mybir.dt.float32
BF16 = mybir.dt.bfloat16
I32 = mybir.dt.int32
U32 = mybir.dt.uint32
U16 = mybir.dt.uint16
U8 = mybir.dt.uint8
E4M3 = mybir.dt.float8_e4m3fn_x4
E5M2 = mybir.dt.float8_e5m2_x4
ALU = mybir.AluOpType
COPY = mybir.ActivationFunctionType.Copy

P = 128
PACK = 4
HALVES = 2
LIST_ROWS = 16
QUADRANTS = 4
STEP = 0.05
STORE_COLUMNS = 512


def tile_list_directions_over_errors_placed_kernel(
    tc, xf, ra, lo, gt, rb, pr, fkr, dr_words, dr_scales, old, offs, offs2, offs3, out
):
    nc = tc.nc
    with ExitStack() as ctx:
        sbuf = ctx.enter_context(tc.tile_pool(name="sbuf", bufs=1))
        psum = ctx.enter_context(tc.psum_pool(name="psum", bufs=1))

        def tile(name, columns, dtype, tag=None, bufs=1):
            return sbuf.tile([P, columns], dtype, name=name, tag=tag or name, bufs=bufs, align_bytes=64)

        def bank(name, tag):
            return psum.tile([P, PACK, P], F32, name=name, tag=tag)

        def load(name, columns, dtype, source, queue=nc.sync):
            loaded = tile(name, columns, dtype)
            queue.dma_start(out=loaded[:], in_=source)
            return loaded

        def in_fours(ap):
            return ap.rearrange("p (c s) -> p c s", s=PACK)

        def dealt(ap):
            return ap.rearrange("p (s c) -> p c s", s=PACK)

        def per_byte(weights):
            return weights[:].rearrange("p (o s) -> p o s", o=1).to_broadcast([P, P, PACK])

        warm = tile("warm", 2, F32)
        nc.vector.memset(warm[:, 0:1], 0.0)

        identity = tile("identity", P, F32)
        nc.vector.memset(identity[:], 0.0)
        make_identity(nc, identity[:], nomemset=True)
        dr_scale = tile("dr_scale", R, U8)
        nc.vector.memset(dr_scale[:].bitcast(U32), 0)
        placed = [tile("placed%d" % b, Q, F32) for b in range(HALVES)]
        for b in range(HALVES):
            nc.vector.memset(placed[b][:], 0.0)

        fk_col = load("fk_col", PACK, F32, fkr.rearrange("o (m t) -> m (o t)", t=PACK), nc.scalar)
        ra_col = load("ra_col", PACK, F32, ra.rearrange("o (p s) -> p (o s)", s=PACK), nc.scalar)
        lo_col = load("lo_col", PACK, F32, lo.rearrange("(m t) o -> m (t o)", t=PACK), nc.scalar)
        rb_col = load("rb_col", PACK, F32, rb.rearrange("o (p s) -> p (o s)", s=PACK), nc.scalar)
        nc.scalar.activation(warm[:, 1:2], warm[:, 0:1], COPY)
        x_list = load("x_list", J // LIST_ROWS, U16, offs)
        xf_tiles = xf.rearrange("(m t) c -> t m c", t=PACK)
        x_table = [load("x_table%d" % t, T, F32, xf_tiles[t]) for t in range(PACK)]
        g_list = load("g_list", J // LIST_ROWS, U16, offs2)
        g_table = [load("g_table%d" % h, V, F32, gt[h * P : (h + 1) * P, :]) for h in range(HALVES)]
        prediction = [load("prediction%d" % h, J, F32, pr[h * P : (h + 1) * P, :]) for h in range(HALVES)]
        dr_code = load("dr_code", R, I32, dr_words[0].rearrange("p c s -> p (c s)").bitcast(I32))
        for quadrant in range(QUADRANTS):
            nc.sync.dma_start(
                out=dr_scale[32 * quadrant : 32 * quadrant + 4, :].bitcast(I32),
                in_=dr_scales[0, 4 * quadrant : 4 * quadrant + 4, :].bitcast(I32),
            )
        out_list = load("out_list", N // LIST_ROWS, U16, offs3)
        old_rows = [load("old_rows%d" % b, Q, F32, old[b * P : (b + 1) * P, :]) for b in range(HALVES)]

        factor = []
        for t in range(PACK):
            spread = psum.tile([P, P], F32, name="spread%d" % t, tag="bank%d" % t)
            nc.tensor.transpose(spread[:], fk_col[:, t : t + 1].to_broadcast([P, P]), identity[:])
            factor.append(tile("factor%d" % t, P * PACK, F32))
            nc.vector.tensor_tensor(
                in_fours(factor[t][:]),
                spread[:].rearrange("p (m o) -> p m o", o=1).to_broadcast([P, P, PACK]),
                per_byte(ra_col),
                ALU.mult,
            )
        minus_lo = tile("minus_lo", PACK, F32, tag="ra_col")
        nc.vector.tensor_scalar(minus_lo[:], lo_col[:], -1.0, None, ALU.mult)

        def gather(name, table, offsets):
            picked = tile(name, J, F32)
            nc.scalar.activation(picked[:], table[:].indirect(offsets[:]), COPY)
            return picked

        x_picked = [gather("x_picked%d" % t, x_table[t], x_list) for t in range(PACK)]
        g_picked = [gather("g_picked%d" % h, g_table[h], g_list) for h in range(HALVES)]

        def turn(parts, name, tag):
            turned = bank(name, tag)
            for s in range(PACK):
                nc.tensor.transpose(turned[:, s, :], parts[s], identity[:])
            return turned

        def turn_excess(t):
            excess = tile("excess%d" % t, J, F32, tag="dealt", bufs=2)
            nc.vector.tensor_scalar(
                dealt(excess[:]), in_fours(x_picked[t][:]), minus_lo[:, t : t + 1], 0.0, ALU.add, ALU.max
            )
            return turn([excess[:, s * P : (s + 1) * P] for s in range(PACK)], "excess_turned%d" % t, "bank%d" % t)

        def turn_error(h):
            error = tile("error%d" % h, J, F32, tag="dealt", bufs=2)
            nc.vector.tensor_tensor(error[:], g_picked[h][:], prediction[h][:], ALU.subtract)
            return turn([error[:, s::PACK] for s in range(PACK)], "error_turned%d" % h, "bank%d" % h)

        def weigh(turned, weights, name, tag=None):
            rounded = tile(name, P * PACK, BF16, tag=tag)
            nc.vector.tensor_tensor(in_fours(rounded[:]), turned[:].rearrange("p s c -> p c s"), weights, ALU.mult)
            return rounded

        def quantize(rounded, name, fmt):
            code = tile(name + "_code", P, U32)
            scale = tile(name + "_scale", P, U8)
            nc.vector.quantize_mx(out=code[:].bitcast(fmt), scales=scale[:], in_=rounded[:])
            return code[:].bitcast(fmt), scale[:]

        prepare = [lambda t=t: turn_excess(t) for t in range(PACK)] + [lambda h=h: turn_error(h) for h in range(HALVES)]
        turned = [prepare[0](), prepare[1]()]
        u_mx = []
        for t in range(PACK):
            rounded = weigh(turned[t], in_fours(factor[t][:]), "u_rounded%d" % t)
            turned.append(prepare[t + 2]())
            u_mx.append(quantize(rounded, "u%d" % t, E4M3))
        g_mx = []
        for h in range(HALVES):
            rounded = weigh(turned[PACK + h], per_byte(rb_col), "g_rounded%d" % h, tag="g_rounded")
            g_mx.append(quantize(rounded, "g%d" % h, E5M2))

        second_rows = psum.tile([P, N], F32, name="second_rows")
        for h in range(HALVES):
            copy = nc.scalar.copy if h == 0 else nc.vector.tensor_copy
            g_code, g_scale = g_mx[h]
            moment = bank("moment%d" % h, "bank%d" % (PACK - HALVES + h))
            for t in range(PACK):
                u_code, u_scale = u_mx[t]
                nc.tensor.matmul_mx(
                    out=moment[:, t, :], lhsT=u_code, lhsT_scale=u_scale, rhs=g_code, rhs_scale=g_scale,
                    start=True, stop=True,
                )
            w_rounded = tile("w_rounded%d" % h, P * PACK, BF16)
            copy(out=in_fours(w_rounded[:]), in_=moment[:].rearrange("p t n -> p n t"))
            w_code, w_scale = quantize(w_rounded, "w%d" % h, E5M2)
            first_rows = psum.tile([P, P], F32, name="first_rows%d" % h)
            for b, seen in enumerate((first_rows[:], second_rows[:, h * P : (h + 1) * P])):
                nc.tensor.matmul_mx(
                    out=seen,
                    lhsT=dr_code[:, b * P : (b + 1) * P].bitcast(E5M2),
                    lhsT_scale=dr_scale[:, b * P : (b + 1) * P],
                    rhs=w_code, rhs_scale=w_scale, start=True, stop=True,
                )
            first_values = tile("first_values%d" % h, P, F32)
            copy(out=first_values[:], in_=first_rows[:])
            places = placed[0][:].indirect(out_list[:, h * P // LIST_ROWS : (h + 1) * P // LIST_ROWS])
            if h == 0:
                nc.scalar.activation(places, first_values[:], COPY)
            else:
                nc.vector.tensor_copy(places, first_values[:])
        second_values = tile("second_values", N, F32)
        nc.scalar.copy(out=second_values[:], in_=second_rows[:])
        nc.scalar.activation(placed[1][:].indirect(out_list[:]), second_values[:], COPY)

        for b in range(HALVES):
            for first in range(0, Q, STORE_COLUMNS):
                columns = slice(first, first + STORE_COLUMNS)
                result = tile("result%d_%d" % (b, first), STORE_COLUMNS, F32)
                nc.vector.scalar_tensor_tensor(
                    result[:], placed[b][:, columns], STEP, old_rows[b][:, columns], ALU.mult, ALU.add
                )
                nc.sync.dma_start(out=out[b * P : (b + 1) * P, columns], in_=result[:])
